import numpy as np
CORES = [2,3,42,43,82,83,122,123]
N = 8
B, S = 16, 256
def entries(a): return a.T.reshape(-1)
def pack(v, P): return np.ascontiguousarray(np.asarray(v, np.int32).reshape(-1, P).T)
def lists(rng, how):
    Q = rng.integers(0, N * B, N * B)
    if how == "alike": Q[:] = rng.integers(N * B)
    if how == "stay": Q = np.arange(N * B)
    if how == "distinct": Q = rng.permutation(N * B)
    if how == "hotrank": Q = B * int(rng.integers(N)) + rng.integers(0, B, N * B)
    if how == "swap": s = int(rng.integers(1, N)); Q = np.concatenate([B * ((r + s) % N) + rng.permutation(B) for r in range(N)])
    return {"parent": np.broadcast_to(pack(Q, 16), (N, 16, N * B // 16)).copy()}
def setup_inputs(rng):
    return dict({"c": rng.standard_normal((N, 128, B * S), dtype=np.float32)}, **lists(rng, "uniform"))
def setup_inputs_alike(rng):
    d = setup_inputs(rng); d.update(lists(rng, "alike"))
    for k in ("c",): d[k] = (d[k].astype(np.float32) * 1048576.0).astype(d[k].dtype)
    return d
def setup_inputs_distinct(rng):
    d = setup_inputs(rng); d.update(lists(rng, "distinct"))
    for k in ("c",): d[k] = (d[k].astype(np.float32) * (1 / 1024.0)).astype(d[k].dtype)
    return d
def setup_inputs_hotrank(rng):
    d = setup_inputs(rng); d.update(lists(rng, "hotrank"))
    return d
def setup_inputs_stay(rng):
    d = setup_inputs(rng); d.update(lists(rng, "stay"))
    return d
def setup_inputs_swap(rng):
    d = setup_inputs(rng); d.update(lists(rng, "swap"))
    return d
def check_inputs(x):
    bad = []
    if x["parent"].min() < 0 or x["parent"].max() >= N * B: bad.append("parent out of range")
    if not all(np.array_equal(a, x["parent"][0]) for a in x["parent"]): bad.append("parent isn't alike on all ranks")
    return bad
def reference(c, parent):
    A = np.concatenate(list(c), axis=1).reshape(128, N * B, S)
    Y = A[:, entries(parent[0]), :]
    return {"y": np.stack([Y[:, B * r:B * r + B].reshape(128, B * S) for r in range(N)])}

@@ -1,0 +1,178 @@
+from concourse.bass import DstId, RemoteDMATransfer
+from concourse.mybir import AluOpType
+
+SIM_CORES = 128
+NR, NB, S = 8, 16, 256
+NV = 16
+W = 256
+
+SCRATCH = {
+    "stage": ("dram", [NV, 128, W], "float32"),
+    "land": ("dram", [NV, 128, W], "float32"),
+    "pd": ("dram", [128, 2], "int32"),
+    "rep": ("sbuf", [128, NR], "int32"),
+    "hi": ("sbuf", [128, NR], "int32"),
+    "hif": ("sbuf", [128, NR], "float32"),
+    "repf": ("sbuf", [128, NR], "float32"),
+    "base": ("sbuf", [128, NR], "float32"),
+    "ramp": ("sbuf", [128, 16], "float32"),
+    "off": ("sbuf", [128, 16 * NR], "uint16"),
+    "lin": ("sbuf", [128, NR * W], "float32"),
+    "win": ("sbuf", [128, NR * W], "float32"),
+    "gat": ("sbuf", [128, NR * W], "float32"),
+    "outb": ("sbuf", [128, NR * W], "float32"),
+}
+SEMAPHORES = (["psem", "pa", "rp", "vi", "vs", "sent", "ys", "yc", "f2", "f3"]
+              + ["ld%d" % k for k in range(4)] + ["a%d" % s for s in range(NR)] + ["r%d" % v for v in range(NV)])
+
+
+def _bits(mask):
+    return [b for b in range(mask.bit_length()) if (mask >> b) & 1]
+
+
+def _mask(engines):
+    m = 0
+    for e in engines:
+        m |= 1 << e
+    return m
+
+
+def _plan(T, topo):
+    ranks = list(T.cores)
+    cores = list(range(SIM_CORES))
+    allchips = sorted({topo.chip(c) for c in cores})
+    chips = []
+    for r in ranks:
+        if topo.chip(r) not in chips:
+            chips.append(topo.chip(r))
+    sorter = {}
+    for q, ch in enumerate(chips):
+        rdie = topo.die([r for r in ranks if topo.chip(r) == ch][0])
+        mate = [x for x in allchips if topo.mates(ch, x)][0]
+        cand = [c for c in cores if topo.chip(c) == mate and c not in ranks
+                and all(topo.may_write(c, r) for r in ranks)]
+        slots = [c for c in cand if topo.die(c) == rdie][:2] + [c for c in cand if topo.die(c) != rdie][:2]
+        for k, c in enumerate(slots):
+            sorter[4 * k + q] = c
+    fwd = {}
+    for ch in chips:
+        here = [r for r in ranks if topo.chip(r) == ch]
+        rdie = topo.die(here[0])
+        helpers = [c for c in cores if topo.chip(c) == ch and c not in ranks and topo.die(c) != rdie
+                   and all(topo.may_write(c, sorter[v]) for v in sorter)]
+        for e, r in enumerate(here):
+            fwd[r] = helpers[e]
+    return ranks, chips, sorter, fwd
+
+
+def _tr(topo, dst, src_ap, dst_ap, engines, sem):
+    rid, pid, _ = topo.addr(dst)
+    return RemoteDMATransfer(dst_ids=[DstId(rid=rid, pnc=pid)], dma_engine_mask=_mask(engines), remote_sem=sem,
+                             src=src_ap, dst=dst_ap)
+
+
+def _rank(g, core, T, topo, ranks, chips, sorter, fwd):
+    sem = T.sem
+    s = T.rank_of(core)
+    q = chips.index(topo.chip(core))
+    e = [r for r in ranks if topo.chip(r) == topo.chip(core)].index(core)
+    lo = _bits(topo.mask(core, sorter[0]))
+    hi = [b for b in _bits(topo.mask(core, fwd[core])) if b not in lo]
+    sent = 0
+    g.sync.dma_start(T.pd[0:64, :], T.parent[:, :]).then_inc(sem.psem, 16)
+    g.sync.dma_start(T.pd[64:128, :], T.parent[:, :]).then_inc(sem.psem, 16)
+    order = (2, 0, 3, 1)
+    for k in order:
+        g.sync.dma_start(T.stage[4 * k:4 * k + 4], T.c[32 * k:32 * k + 32, :]).then_inc(sem["ld%d" % k], 16)
+    g.wait_ge(sem.psem, 32)
+    g.remote_dma_fused([_tr(topo, sorter[4 * (2 * i + e) + q], T.pd[:], T.pd[:], lo[i:i + 1], sem.pa) for i in range(2)],
+                       local_sem=sem.sent)
+    sent += 2
+    for k in order:
+        g.wait_ge(sem["ld%d" % k], 16)
+        if k >= 2:
+            trs = [_tr(topo, fwd[core], T.stage[4 * k + i], T.stage[4 * k + i], hi[2 * i:2 * i + 2], sem["f%d" % k])
+                   for i in range(4)]
+        else:
+            trs = [_tr(topo, sorter[4 * k + (q + i) % 4], T.stage[4 * k + (q + i) % 4], T.lin[:, W * s:W * s + W],
+                       lo[2 * i:2 * i + 2], sem["a%d" % s]) for i in range(4)]
+        g.remote_dma_fused(trs, local_sem=sem.sent)
+        sent += 8
+    for queue, ks, done in ((g.sync, (0, 1), sem.ys), (g.scalar, (2, 3), sem.yc)):
+        for k in ks:
+            for i in range(4):
+                v = 4 * k + (q - i) % 4
+                queue.wait_ge(sem["r%d" % v], 4)
+                queue.dma_start(T.y[8 * v:8 * v + 8, :], T.land[v]).then_inc(done, 16)
+        queue.wait_ge(done, 16 * 8)
+    g.wait_ge(sem.sent, sent)
+
+
+def _forwarder(g, core, T, topo, ranks, chips, sorter, fwd):
+    sem = T.sem
+    r = [x for x in ranks if fwd[x] == core][0]
+    s = T.rank_of(r)
+    q = chips.index(topo.chip(core))
+    lo = _bits(topo.mask(core, sorter[0]))
+    sent = 0
+    for k in (2, 3):
+        g.wait_ge(sem["f%d" % k], 8)
+        g.remote_dma_fused([_tr(topo, sorter[4 * k + (q + i) % 4], T.stage[4 * k + (q + i) % 4], T.lin[:, W * s:W * s + W],
+                                lo[2 * i:2 * i + 2], sem["a%d" % s]) for i in range(4)], local_sem=sem.sent)
+        sent += 8
+    g.wait_ge(sem.sent, sent)
+
+
+def _sorter(g, core, T, topo, ranks, chips, sorter):
+    sem = T.sem
+    v = [x for x in sorter if sorter[x] == core][0]
+    q = v % 4
+    lo = _bits(topo.mask(core, ranks[0]))
+    n = [0]
+
+    def vop(make):
+        if n[0]:
+            g.vector.wait_ge(sem.vs, n[0])
+        make().then_inc(sem.vs, 1)
+        n[0] += 1
+
+    g.iota(T.ramp[:, :], [[16, 16]], 0, 0, allow_small_or_imprecise_dtypes=True).then_inc(sem.vi, 1)
+    for i, queue in enumerate((g.sync, g.scalar)):
+        queue.wait_ge(sem.pa, 1)
+        for grp in range(4 * i, 4 * i + 4):
+            queue.dma_start(T.rep[16 * grp:16 * grp + 16, :], T.pd[0:64, :]).then_inc(sem.rp, 16)
+    g.vector.wait_ge(sem.rp, 16 * 8)
+    g.vector.wait_ge(sem.vi, 1)
+    vop(lambda: g.vector.tensor_scalar(T.hi[:, :], T.rep[:, :], 4, None, AluOpType.arith_shift_right))
+    vop(lambda: g.vector.tensor_copy(T.repf[:, :], T.rep[:, :]))
+    vop(lambda: g.vector.tensor_scalar(T.hif[:, :], T.hi[:, :], W - NB, None, AluOpType.mult))
+    vop(lambda: g.vector.tensor_tensor(T.base[:, :], T.hif[:, :], T.repf[:, :], AluOpType.add))
+    for d in range(NR):
+        vop(lambda: g.vector.tensor_scalar(T.off[:, 16 * d:16 * d + 16], T.ramp[:, :], T.base[:, d:d + 1], None,
+                                           AluOpType.add))
+    for s in range(NR):
+        g.vector.wait_ge(sem["a%d" % s], 2)
+        vop(lambda: g.vector.transpose(T.win[:, W * s:W * s + W], T.lin[:, W * s:W * s + W]))
+    sent = 0
+    for i in range(4):
+        ch = chips[(q + i) % 4]
+        ds = [T.rank_of(r) for r in ranks if topo.chip(r) == ch]
+        for d in ds:
+            vop(lambda: g.vector.tensor_copy(T.gat[:, W * d:W * d + W],
+                                             T.win[:, 0:NR * W].indirect(T.off[:, 16 * d:16 * d + 16])))
+            vop(lambda: g.vector.transpose(T.outb[:, W * d:W * d + W], T.gat[:, W * d:W * d + W]))
+        g.wait_ge(sem.vs, n[0])
+        g.remote_dma_fused([_tr(topo, ranks[d], T.outb[:, W * d:W * d + W], T.land[v], lo[4 * j:4 * j + 4],
+                                sem["r%d" % v]) for j, d in enumerate(ds)], local_sem=sem.sent)
+        sent += 8
+    g.wait_ge(sem.sent, sent)
+
+
+def rank_program(g, core, T, topo):
+    ranks, chips, sorter, fwd = _plan(T, topo)
+    if core in ranks:
+        _rank(g, core, T, topo, ranks, chips, sorter, fwd)
+    elif core in fwd.values():
+        _forwarder(g, core, T, topo, ranks, chips, sorter, fwd)
+    elif core in sorter.values():
+        _sorter(g, core, T, topo, ranks, chips, sorter)

@@ -5,11 +5,11 @@ SIM_CORES = 128
 NR, NB, S = 8, 16, 256
 NV = 16
 W = 256
+HW = NR // 2
 
 SCRATCH = {
     "stage": ("dram", [NV, 128, W], "float32"),
     "land": ("dram", [NV, 128, W], "float32"),
-    "pd": ("dram", [128, 2], "int32"),
     "rep": ("sbuf", [128, NR], "int32"),
     "hi": ("sbuf", [128, NR], "int32"),
     "hif": ("sbuf", [128, NR], "float32"),
@@ -22,8 +22,9 @@ SCRATCH = {
     "gat": ("sbuf", [128, NR * W], "float32"),
     "outb": ("sbuf", [128, NR * W], "float32"),
 }
-SEMAPHORES = (["psem", "pa", "rp", "vi", "vs", "sent", "ys", "yc", "f2", "f3"]
-              + ["ld%d" % k for k in range(4)] + ["a%d" % s for s in range(NR)] + ["r%d" % v for v in range(NV)])
+SEMAPHORES = (["psem", "pa", "pb", "vi", "vs", "vo", "vw", "sent", "ys", "yc", "go", "go2"]
+              + ["f%d" % k for k in range(4)] + ["ld%d" % k for k in range(4)] + ["a%d" % s for s in range(NR)]
+              + ["r%d" % v for v in range(NV)] + ["gd%d" % d for d in range(NR)] + ["td%d" % d for d in range(NR)])
 
 
 def _bits(mask):
@@ -45,16 +46,16 @@ def _plan(T, topo):
     for r in ranks:
         if topo.chip(r) not in chips:
             chips.append(topo.chip(r))
-    sorter = {}
+    sorter, slots = {}, {}
     for q, ch in enumerate(chips):
         rdie = topo.die([r for r in ranks if topo.chip(r) == ch][0])
         mate = [x for x in allchips if topo.mates(ch, x)][0]
         cand = [c for c in cores if topo.chip(c) == mate and c not in ranks
                 and all(topo.may_write(c, r) for r in ranks)]
-        slots = [c for c in cand if topo.die(c) == rdie][:2] + [c for c in cand if topo.die(c) != rdie][:2]
-        for k, c in enumerate(slots):
-            sorter[4 * k + q] = c
-    fwd = {}
+        slots[q] = [c for c in cand if topo.die(c) == rdie][:2] + [c for c in cand if topo.die(c) != rdie][:2]
+        for k in range(4):
+            sorter[4 * k + q] = slots[q][2 * ((k + q) % 2) + k // 2]
+    via, fwd = {}, {}
     for ch in chips:
         here = [r for r in ranks if topo.chip(r) == ch]
         rdie = topo.die(here[0])
@@ -62,7 +63,11 @@ def _plan(T, topo):
                    and all(topo.may_write(c, sorter[v]) for v in sorter)]
         for e, r in enumerate(here):
             fwd[r] = helpers[e]
-    return ranks, chips, sorter, fwd
+            via[r] = {}
+            for k in range(4):
+                for q in range(4):
+                    via[r][4 * k + q] = r if (k + q + e) % 2 == 0 else helpers[e]
+    return ranks, chips, sorter, slots, via, fwd
 
 
 def _tr(topo, dst, src_ap, dst_ap, engines, sem):
@@ -71,7 +76,7 @@ def _tr(topo, dst, src_ap, dst_ap, engines, sem):
                              src=src_ap, dst=dst_ap)
 
 
-def _rank(g, core, T, topo, ranks, chips, sorter, fwd):
+def _rank(g, core, T, topo, ranks, chips, sorter, slots, via, fwd):
     sem = T.sem
     s = T.rank_of(core)
     q = chips.index(topo.chip(core))
@@ -79,28 +84,40 @@ def _rank(g, core, T, topo, ranks, chips, sorter, fwd):
     lo = _bits(topo.mask(core, sorter[0]))
     hi = [b for b in _bits(topo.mask(core, fwd[core])) if b not in lo]
     sent = 0
-    g.sync.dma_start(T.pd[0:64, :], T.parent[:, :]).then_inc(sem.psem, 16)
-    g.sync.dma_start(T.pd[64:128, :], T.parent[:, :]).then_inc(sem.psem, 16)
-    order = (2, 0, 3, 1)
-    for k in order:
+    for grp in range(8):
+        (g.sync, g.scalar)[grp % 2].dma_start(T.rep[16 * grp:16 * grp + 16, HW * e:HW * e + HW],
+                                              T.parent[:, HW * e:HW * e + HW]).then_inc(sem.psem, 16)
+
+    def load(k):
         g.sync.dma_start(T.stage[4 * k:4 * k + 4], T.c[32 * k:32 * k + 32, :]).then_inc(sem["ld%d" % k], 16)
-    g.wait_ge(sem.psem, 32)
-    g.remote_dma_fused([_tr(topo, sorter[4 * (2 * i + e) + q], T.pd[:], T.pd[:], lo[i:i + 1], sem.pa) for i in range(2)],
-                       local_sem=sem.sent)
-    sent += 2
-    for k in order:
+
+    load(0)
+    load(1)
+    g.sync.wait_ge(sem.go, 1)
+    load(2)
+    load(3)
+    g.sync.sem_inc(sem.go2, 1)
+    g.wait_ge(sem.psem, 16 * 8)
+    half = T.rep[:, HW * e:HW * e + HW]
+    g.remote_dma_fused([_tr(topo, slots[q][e], half, half, lo, sem.pa),
+                        _tr(topo, fwd[core], half, half, hi, sem.pa)], local_sem=sem.sent)
+    sent += 16
+    for k in range(4):
         g.wait_ge(sem["ld%d" % k], 16)
-        if k >= 2:
-            trs = [_tr(topo, fwd[core], T.stage[4 * k + i], T.stage[4 * k + i], hi[2 * i:2 * i + 2], sem["f%d" % k])
-                   for i in range(4)]
-        else:
-            trs = [_tr(topo, sorter[4 * k + (q + i) % 4], T.stage[4 * k + (q + i) % 4], T.lin[:, W * s:W * s + W],
-                       lo[2 * i:2 * i + 2], sem["a%d" % s]) for i in range(4)]
-        g.remote_dma_fused(trs, local_sem=sem.sent)
-        sent += 8
-    for queue, ks, done in ((g.sync, (0, 1), sem.ys), (g.scalar, (2, 3), sem.yc)):
-        for k in ks:
-            for i in range(4):
+        vs = [4 * k + (q + i) % 4 for i in range(4)]
+        far = [v for v in vs if via[core][v] != core]
+        near = [v for v in vs if via[core][v] == core]
+        g.remote_dma_fused([_tr(topo, fwd[core], T.stage[v], T.stage[v], hi[4 * i:4 * i + 4], sem["f%d" % k])
+                            for i, v in enumerate(far)]
+                           + [_tr(topo, sorter[v], T.stage[v], T.lin[:, W * s:W * s + W], lo[4 * i:4 * i + 4],
+                                  sem["a%d" % s]) for i, v in enumerate(near)], local_sem=sem.sent)
+        sent += 16
+        if k == 0:
+            g.sem_inc(sem.go, 1)
+            g.wait_ge(sem.go2, 1)
+    for queue, turn, done in ((g.sync, 0, sem.ys), (g.scalar, 1, sem.yc)):
+        for k in range(4):
+            for i in (turn, turn + 2):
                 v = 4 * k + (q - i) % 4
                 queue.wait_ge(sem["r%d" % v], 4)
                 queue.dma_start(T.y[8 * v:8 * v + 8, :], T.land[v]).then_inc(done, 16)
@@ -108,60 +125,70 @@ def _rank(g, core, T, topo, ranks, chips, sorter, fwd):
     g.wait_ge(sem.sent, sent)
 
 
-def _forwarder(g, core, T, topo, ranks, chips, sorter, fwd):
+def _forwarder(g, core, T, topo, ranks, chips, sorter, slots, via, fwd):
     sem = T.sem
     r = [x for x in ranks if fwd[x] == core][0]
     s = T.rank_of(r)
     q = chips.index(topo.chip(core))
+    e = [x for x in ranks if topo.chip(x) == topo.chip(core)].index(r)
     lo = _bits(topo.mask(core, sorter[0]))
     sent = 0
-    for k in (2, 3):
+    half = T.rep[:, HW * e:HW * e + HW]
+    g.wait_ge(sem.pa, 8)
+    g.remote_dma_fused([_tr(topo, slots[q][2 + e], half, half, lo, sem.pa)], local_sem=sem.sent)
+    sent += 8
+    for k in range(4):
+        far = [4 * k + (q + i) % 4 for i in range(4) if via[r][4 * k + (q + i) % 4] == core]
         g.wait_ge(sem["f%d" % k], 8)
-        g.remote_dma_fused([_tr(topo, sorter[4 * k + (q + i) % 4], T.stage[4 * k + (q + i) % 4], T.lin[:, W * s:W * s + W],
-                                lo[2 * i:2 * i + 2], sem["a%d" % s]) for i in range(4)], local_sem=sem.sent)
+        g.remote_dma_fused([_tr(topo, sorter[v], T.stage[v], T.lin[:, W * s:W * s + W], lo[4 * i:4 * i + 4],
+                                sem["a%d" % s]) for i, v in enumerate(far)], local_sem=sem.sent)
         sent += 8
     g.wait_ge(sem.sent, sent)
 
 
-def _sorter(g, core, T, topo, ranks, chips, sorter):
+def _sorter(g, core, T, topo, ranks, chips, sorter, slots, via):
     sem = T.sem
     v = [x for x in sorter if sorter[x] == core][0]
     q = v % 4
     lo = _bits(topo.mask(core, ranks[0]))
-    n = [0]
-
-    def vop(make):
-        if n[0]:
-            g.vector.wait_ge(sem.vs, n[0])
-        make().then_inc(sem.vs, 1)
-        n[0] += 1
-
+    vec = g.vector
     g.iota(T.ramp[:, :], [[16, 16]], 0, 0, allow_small_or_imprecise_dtypes=True).then_inc(sem.vi, 1)
-    for i, queue in enumerate((g.sync, g.scalar)):
-        queue.wait_ge(sem.pa, 1)
-        for grp in range(4 * i, 4 * i + 4):
-            queue.dma_start(T.rep[16 * grp:16 * grp + 16, :], T.pd[0:64, :]).then_inc(sem.rp, 16)
-    g.vector.wait_ge(sem.rp, 16 * 8)
-    g.vector.wait_ge(sem.vi, 1)
-    vop(lambda: g.vector.tensor_scalar(T.hi[:, :], T.rep[:, :], 4, None, AluOpType.arith_shift_right))
-    vop(lambda: g.vector.tensor_copy(T.repf[:, :], T.rep[:, :]))
-    vop(lambda: g.vector.tensor_scalar(T.hif[:, :], T.hi[:, :], W - NB, None, AluOpType.mult))
-    vop(lambda: g.vector.tensor_tensor(T.base[:, :], T.hif[:, :], T.repf[:, :], AluOpType.add))
+    sl = slots[q].index(core)
+    e = sl % 2
+    half = T.rep[:, HW * e:HW * e + HW]
+    g.wait_ge(sem.pa, 8)
+    g.remote_dma_fused([_tr(topo, slots[q][sl - e + 1 - e], half, half, lo, sem.pb)], local_sem=sem.sent)
+    sent = 8
+    vec.wait_ge(sem.pa, 8)
+    vec.wait_ge(sem.pb, 8)
+    vec.wait_ge(sem.vi, 1)
+    vec.tensor_scalar(T.hi[:, :], T.rep[:, :], 4, None, AluOpType.arith_shift_right).then_inc(sem.vs, 1)
+    vec.tensor_copy(T.repf[:, :], T.rep[:, :]).then_inc(sem.vs, 1)
+    vec.wait_ge(sem.vs, 2)
+    vec.tensor_scalar(T.hif[:, :], T.hi[:, :], W - NB, None, AluOpType.mult).then_inc(sem.vs, 1)
+    vec.wait_ge(sem.vs, 3)
+    vec.tensor_tensor(T.base[:, :], T.hif[:, :], T.repf[:, :], AluOpType.add).then_inc(sem.vs, 1)
+    vec.wait_ge(sem.vs, 4)
     for d in range(NR):
-        vop(lambda: g.vector.tensor_scalar(T.off[:, 16 * d:16 * d + 16], T.ramp[:, :], T.base[:, d:d + 1], None,
-                                           AluOpType.add))
-    for s in range(NR):
-        g.vector.wait_ge(sem["a%d" % s], 2)
-        vop(lambda: g.vector.transpose(T.win[:, W * s:W * s + W], T.lin[:, W * s:W * s + W]))
-    sent = 0
+        vec.tensor_scalar(T.off[:, 16 * d:16 * d + 16], T.ramp[:, :], T.base[:, d:d + 1], None,
+                          AluOpType.add).then_inc(sem.vo, 1)
+    for r in sorted(ranks, key=lambda x: (via[x][v] != x, T.rank_of(x))):
+        s = T.rank_of(r)
+        vec.wait_ge(sem["a%d" % s], 4)
+        vec.transpose(T.win[:, W * s:W * s + W], T.lin[:, W * s:W * s + W]).then_inc(sem.vw, 1)
+    vec.wait_ge(sem.vo, NR)
+    vec.wait_ge(sem.vw, NR)
     for i in range(4):
         ch = chips[(q + i) % 4]
         ds = [T.rank_of(r) for r in ranks if topo.chip(r) == ch]
         for d in ds:
-            vop(lambda: g.vector.tensor_copy(T.gat[:, W * d:W * d + W],
-                                             T.win[:, 0:NR * W].indirect(T.off[:, 16 * d:16 * d + 16])))
-            vop(lambda: g.vector.transpose(T.outb[:, W * d:W * d + W], T.gat[:, W * d:W * d + W]))
-        g.wait_ge(sem.vs, n[0])
+            vec.tensor_copy(T.gat[:, W * d:W * d + W],
+                            T.win[:, 0:NR * W].indirect(T.off[:, 16 * d:16 * d + 16])).then_inc(sem["gd%d" % d], 1)
+        for d in ds:
+            vec.wait_ge(sem["gd%d" % d], 1)
+            vec.transpose(T.outb[:, W * d:W * d + W], T.gat[:, W * d:W * d + W]).then_inc(sem["td%d" % d], 1)
+        for d in ds:
+            g.wait_ge(sem["td%d" % d], 1)
         g.remote_dma_fused([_tr(topo, ranks[d], T.outb[:, W * d:W * d + W], T.land[v], lo[4 * j:4 * j + 4],
                                 sem["r%d" % v]) for j, d in enumerate(ds)], local_sem=sem.sent)
         sent += 8
@@ -169,10 +196,10 @@ def _sorter(g, core, T, topo, ranks, chips, sorter):
 
 
 def rank_program(g, core, T, topo):
-    ranks, chips, sorter, fwd = _plan(T, topo)
+    ranks, chips, sorter, slots, via, fwd = _plan(T, topo)
     if core in ranks:
-        _rank(g, core, T, topo, ranks, chips, sorter, fwd)
+        _rank(g, core, T, topo, ranks, chips, sorter, slots, via, fwd)
     elif core in fwd.values():
-        _forwarder(g, core, T, topo, ranks, chips, sorter, fwd)
+        _forwarder(g, core, T, topo, ranks, chips, sorter, slots, via, fwd)
     elif core in sorter.values():
-        _sorter(g, core, T, topo, ranks, chips, sorter)
+        _sorter(g, core, T, topo, ranks, chips, sorter, slots, via)

@@ -3,28 +3,36 @@ from concourse.mybir import AluOpType
 
 SIM_CORES = 128
 NR, NB, S = 8, 16, 256
-NV = 16
-W = 256
+NV = 32
+RD = NV // 4
+W = 128
+JW = NR * W
 HW = NR // 2
 
 SCRATCH = {
     "stage": ("dram", [NV, 128, W], "float32"),
     "land": ("dram", [NV, 128, W], "float32"),
-    "rep": ("sbuf", [128, NR], "int32"),
-    "hi": ("sbuf", [128, NR], "int32"),
-    "hif": ("sbuf", [128, NR], "float32"),
-    "repf": ("sbuf", [128, NR], "float32"),
-    "base": ("sbuf", [128, NR], "float32"),
-    "ramp": ("sbuf", [128, 16], "float32"),
-    "off": ("sbuf", [128, 16 * NR], "uint16"),
-    "lin": ("sbuf", [128, NR * W], "float32"),
-    "win": ("sbuf", [128, NR * W], "float32"),
-    "gat": ("sbuf", [128, NR * W], "float32"),
-    "outb": ("sbuf", [128, NR * W], "float32"),
+    "rep": ("sbuf", [128, 2 * NR], "int32"),
+    "hi": ("sbuf", [128, 2 * NR], "int32"),
+    "hif": ("sbuf", [128, 2 * NR], "float32"),
+    "repf": ("sbuf", [128, 2 * NR], "float32"),
+    "base": ("sbuf", [128, 2 * NR], "float32"),
+    "pidx": ("sbuf", [128, 4], "int32"),
+    "pbit": ("sbuf", [128, 4], "int32"),
+    "pbf": ("sbuf", [128, 4], "float32"),
+    "ramp": ("sbuf", [128, 4], "float32"),
+    "ramp2": ("sbuf", [128, 4], "float32"),
+    "off": ("sbuf", [128, 8 * NR], "uint16"),
+    "lin": ("sbuf", [128, 2 * JW], "float32"),
+    "win": ("sbuf", [128, 2 * JW], "float32"),
+    "gat": ("sbuf", [128, 2 * JW], "float32"),
+    "outb": ("sbuf", [128, 2 * JW], "float32"),
 }
-SEMAPHORES = (["psem", "pa", "pb", "vi", "vs", "vo", "vw", "sent", "ys", "yc", "go", "go2"]
-              + ["f%d" % k for k in range(4)] + ["ld%d" % k for k in range(4)] + ["a%d" % s for s in range(NR)]
-              + ["r%d" % v for v in range(NV)] + ["gd%d" % d for d in range(NR)] + ["td%d" % d for d in range(NR)])
+SEMAPHORES = (["psem", "pa", "pb", "vi", "vp", "vs", "vo", "vw0", "vw1", "sent", "ys", "yc", "go", "go2"]
+              + ["f%d" % k for k in range(RD)] + ["ld%d" % k for k in range(RD)]
+              + ["a%d_%d" % (b, s) for b in range(2) for s in range(NR)] + ["r%d" % v for v in range(NV)]
+              + ["gd%d_%d" % (b, d) for b in range(2) for d in range(NR)]
+              + ["td%d_%d" % (b, d) for b in range(2) for d in range(NR)])
 
 
 def _bits(mask):
@@ -53,8 +61,9 @@ def _plan(T, topo):
         cand = [c for c in cores if topo.chip(c) == mate and c not in ranks
                 and all(topo.may_write(c, r) for r in ranks)]
         slots[q] = [c for c in cand if topo.die(c) == rdie][:2] + [c for c in cand if topo.die(c) != rdie][:2]
-        for k in range(4):
-            sorter[4 * k + q] = slots[q][2 * ((k + q) % 2) + k // 2]
+        for i in range(RD):
+            k = i % 4
+            sorter[4 * i + q] = slots[q][2 * ((k + q) % 2) + k // 2]
     via, fwd = {}, {}
     for ch in chips:
         here = [r for r in ranks if topo.chip(r) == ch]
@@ -64,9 +73,9 @@ def _plan(T, topo):
         for e, r in enumerate(here):
             fwd[r] = helpers[e]
             via[r] = {}
-            for k in range(4):
+            for i in range(RD):
                 for q in range(4):
-                    via[r][4 * k + q] = r if (k + q + e) % 2 == 0 else helpers[e]
+                    via[r][4 * i + q] = r if (i + q + e) % 2 == 0 else helpers[e]
     return ranks, chips, sorter, slots, via, fwd
 
 
@@ -74,6 +83,11 @@ def _tr(topo, dst, src_ap, dst_ap, engines, sem):
     rid, pid, _ = topo.addr(dst)
     return RemoteDMATransfer(dst_ids=[DstId(rid=rid, pnc=pid)], dma_engine_mask=_mask(engines), remote_sem=sem,
                              src=src_ap, dst=dst_ap)
+
+
+def _lin(T, v, s):
+    a = JW * (v // (NV // 2)) + W * s
+    return T.lin[:, a:a + W]
 
 
 def _rank(g, core, T, topo, ranks, chips, sorter, slots, via, fwd):
@@ -84,44 +98,49 @@ def _rank(g, core, T, topo, ranks, chips, sorter, slots, via, fwd):
     lo = _bits(topo.mask(core, sorter[0]))
     hi = [b for b in _bits(topo.mask(core, fwd[core])) if b not in lo]
     sent = 0
+    n = 0
     for grp in range(8):
-        (g.sync, g.scalar)[grp % 2].dma_start(T.rep[16 * grp:16 * grp + 16, HW * e:HW * e + HW],
-                                              T.parent[:, HW * e:HW * e + HW]).then_inc(sem.psem, 16)
+        for t in range(2):
+            for two in range(2):
+                (g.sync, g.scalar)[n % 2].dma_start(
+                    T.rep[16 * grp + two:16 * grp + 16:2, 2 * HW * e + HW * t:2 * HW * e + HW * t + HW],
+                    T.parent[8 * t:8 * t + 8, HW * e:HW * e + HW]).then_inc(sem.psem, 16)
+                n += 1
 
-    def load(k):
-        g.sync.dma_start(T.stage[4 * k:4 * k + 4], T.c[32 * k:32 * k + 32, :]).then_inc(sem["ld%d" % k], 16)
+    def load(i):
+        g.sync.dma_start(T.stage[4 * i:4 * i + 4], T.c[16 * i:16 * i + 16, :]).then_inc(sem["ld%d" % i], 16)
 
-    load(0)
-    load(1)
+    for i in range(RD // 2):
+        load(i)
     g.sync.wait_ge(sem.go, 1)
-    load(2)
-    load(3)
+    for i in range(RD // 2, RD):
+        load(i)
     g.sync.sem_inc(sem.go2, 1)
-    g.wait_ge(sem.psem, 16 * 8)
-    half = T.rep[:, HW * e:HW * e + HW]
+    g.wait_ge(sem.psem, 16 * n)
+    half = T.rep[:, 2 * HW * e:2 * HW * e + 2 * HW]
     g.remote_dma_fused([_tr(topo, slots[q][e], half, half, lo, sem.pa),
                         _tr(topo, fwd[core], half, half, hi, sem.pa)], local_sem=sem.sent)
     sent += 16
-    for k in range(4):
-        g.wait_ge(sem["ld%d" % k], 16)
-        vs = [4 * k + (q + i) % 4 for i in range(4)]
+    for i in range(RD):
+        g.wait_ge(sem["ld%d" % i], 16)
+        vs = [4 * i + (q + j) % 4 for j in range(4)]
         far = [v for v in vs if via[core][v] != core]
         near = [v for v in vs if via[core][v] == core]
-        g.remote_dma_fused([_tr(topo, fwd[core], T.stage[v], T.stage[v], hi[4 * i:4 * i + 4], sem["f%d" % k])
-                            for i, v in enumerate(far)]
-                           + [_tr(topo, sorter[v], T.stage[v], T.lin[:, W * s:W * s + W], lo[4 * i:4 * i + 4],
-                                  sem["a%d" % s]) for i, v in enumerate(near)], local_sem=sem.sent)
+        g.remote_dma_fused([_tr(topo, fwd[core], T.stage[v], T.stage[v], hi[4 * j:4 * j + 4], sem["f%d" % i])
+                            for j, v in enumerate(far)]
+                           + [_tr(topo, sorter[v], T.stage[v], _lin(T, v, s), lo[4 * j:4 * j + 4],
+                                  sem["a%d_%d" % (v // (NV // 2), s)]) for j, v in enumerate(near)], local_sem=sem.sent)
         sent += 16
-        if k == 0:
+        if i == 1:
             g.sem_inc(sem.go, 1)
             g.wait_ge(sem.go2, 1)
-    for queue, turn, done in ((g.sync, 0, sem.ys), (g.scalar, 1, sem.yc)):
-        for k in range(4):
-            for i in (turn, turn + 2):
-                v = 4 * k + (q - i) % 4
-                queue.wait_ge(sem["r%d" % v], 4)
-                queue.dma_start(T.y[8 * v:8 * v + 8, :], T.land[v]).then_inc(done, 16)
-        queue.wait_ge(done, 16 * 8)
+    for queue, z, done in ((g.sync, 0, sem.ys), (g.scalar, 1, sem.yc)):
+        for i in range(RD):
+            a = 4 * i + 2 * z
+            queue.wait_ge(sem["r%d" % a], 4)
+            queue.wait_ge(sem["r%d" % (a + 1)], 4)
+            queue.dma_start(T.y[4 * a:4 * a + 8, :], T.land[a:a + 2]).then_inc(done, 16)
+        queue.wait_ge(done, 16 * RD)
     g.wait_ge(sem.sent, sent)
 
 
@@ -133,65 +152,78 @@ def _forwarder(g, core, T, topo, ranks, chips, sorter, slots, via, fwd):
     e = [x for x in ranks if topo.chip(x) == topo.chip(core)].index(r)
     lo = _bits(topo.mask(core, sorter[0]))
     sent = 0
-    half = T.rep[:, HW * e:HW * e + HW]
+    half = T.rep[:, 2 * HW * e:2 * HW * e + 2 * HW]
     g.wait_ge(sem.pa, 8)
     g.remote_dma_fused([_tr(topo, slots[q][2 + e], half, half, lo, sem.pa)], local_sem=sem.sent)
     sent += 8
-    for k in range(4):
-        far = [4 * k + (q + i) % 4 for i in range(4) if via[r][4 * k + (q + i) % 4] == core]
-        g.wait_ge(sem["f%d" % k], 8)
-        g.remote_dma_fused([_tr(topo, sorter[v], T.stage[v], T.lin[:, W * s:W * s + W], lo[4 * i:4 * i + 4],
-                                sem["a%d" % s]) for i, v in enumerate(far)], local_sem=sem.sent)
+    for i in range(RD):
+        far = [4 * i + (q + j) % 4 for j in range(4) if via[r][4 * i + (q + j) % 4] == core]
+        g.wait_ge(sem["f%d" % i], 8)
+        g.remote_dma_fused([_tr(topo, sorter[v], T.stage[v], _lin(T, v, s), lo[4 * j:4 * j + 4],
+                                sem["a%d_%d" % (v // (NV // 2), s)]) for j, v in enumerate(far)], local_sem=sem.sent)
         sent += 8
     g.wait_ge(sem.sent, sent)
 
 
 def _sorter(g, core, T, topo, ranks, chips, sorter, slots, via):
     sem = T.sem
-    v = [x for x in sorter if sorter[x] == core][0]
-    q = v % 4
+    mine = sorted(x for x in sorter if sorter[x] == core)
+    q = mine[0] % 4
     lo = _bits(topo.mask(core, ranks[0]))
     vec = g.vector
-    g.iota(T.ramp[:, :], [[16, 16]], 0, 0, allow_small_or_imprecise_dtypes=True).then_inc(sem.vi, 1)
+    g.iota(T.ramp[:, :], [[32, 4]], 0, 0, allow_small_or_imprecise_dtypes=True).then_inc(sem.vi, 1)
+    g.iota(T.pidx[:, :], [[0, 4]], 0, 1).then_inc(sem.vi, 1)
+    vec.wait_ge(sem.vi, 2)
+    vec.tensor_scalar(T.pbit[:, :], T.pidx[:, :], 1, None, AluOpType.bitwise_and).then_inc(sem.vp, 1)
+    vec.wait_ge(sem.vp, 1)
+    vec.tensor_copy(T.pbf[:, :], T.pbit[:, :]).then_inc(sem.vp, 1)
+    vec.wait_ge(sem.vp, 2)
+    vec.tensor_tensor(T.ramp2[:, :], T.ramp[:, :], T.pbf[:, :], AluOpType.add).then_inc(sem.vp, 1)
     sl = slots[q].index(core)
     e = sl % 2
-    half = T.rep[:, HW * e:HW * e + HW]
+    half = T.rep[:, 2 * HW * e:2 * HW * e + 2 * HW]
     g.wait_ge(sem.pa, 8)
     g.remote_dma_fused([_tr(topo, slots[q][sl - e + 1 - e], half, half, lo, sem.pb)], local_sem=sem.sent)
     sent = 8
     vec.wait_ge(sem.pa, 8)
     vec.wait_ge(sem.pb, 8)
-    vec.wait_ge(sem.vi, 1)
     vec.tensor_scalar(T.hi[:, :], T.rep[:, :], 4, None, AluOpType.arith_shift_right).then_inc(sem.vs, 1)
-    vec.tensor_copy(T.repf[:, :], T.rep[:, :]).then_inc(sem.vs, 1)
+    vec.tensor_scalar(T.repf[:, :], T.rep[:, :], 2, None, AluOpType.mult).then_inc(sem.vs, 1)
     vec.wait_ge(sem.vs, 2)
-    vec.tensor_scalar(T.hif[:, :], T.hi[:, :], W - NB, None, AluOpType.mult).then_inc(sem.vs, 1)
+    vec.tensor_scalar(T.hif[:, :], T.hi[:, :], W - 2 * NB, None, AluOpType.mult).then_inc(sem.vs, 1)
     vec.wait_ge(sem.vs, 3)
     vec.tensor_tensor(T.base[:, :], T.hif[:, :], T.repf[:, :], AluOpType.add).then_inc(sem.vs, 1)
     vec.wait_ge(sem.vs, 4)
+    vec.wait_ge(sem.vp, 3)
     for d in range(NR):
-        vec.tensor_scalar(T.off[:, 16 * d:16 * d + 16], T.ramp[:, :], T.base[:, d:d + 1], None,
-                          AluOpType.add).then_inc(sem.vo, 1)
-    for r in sorted(ranks, key=lambda x: (via[x][v] != x, T.rank_of(x))):
-        s = T.rank_of(r)
-        vec.wait_ge(sem["a%d" % s], 4)
-        vec.transpose(T.win[:, W * s:W * s + W], T.lin[:, W * s:W * s + W]).then_inc(sem.vw, 1)
-    vec.wait_ge(sem.vo, NR)
-    vec.wait_ge(sem.vw, NR)
-    for i in range(4):
-        ch = chips[(q + i) % 4]
-        ds = [T.rank_of(r) for r in ranks if topo.chip(r) == ch]
-        for d in ds:
-            vec.tensor_copy(T.gat[:, W * d:W * d + W],
-                            T.win[:, 0:NR * W].indirect(T.off[:, 16 * d:16 * d + 16])).then_inc(sem["gd%d" % d], 1)
-        for d in ds:
-            vec.wait_ge(sem["gd%d" % d], 1)
-            vec.transpose(T.outb[:, W * d:W * d + W], T.gat[:, W * d:W * d + W]).then_inc(sem["td%d" % d], 1)
-        for d in ds:
-            g.wait_ge(sem["td%d" % d], 1)
-        g.remote_dma_fused([_tr(topo, ranks[d], T.outb[:, W * d:W * d + W], T.land[v], lo[4 * j:4 * j + 4],
-                                sem["r%d" % v]) for j, d in enumerate(ds)], local_sem=sem.sent)
-        sent += 8
+        for t in range(2):
+            col = 2 * HW * (d // HW) + HW * t + d % HW
+            vec.tensor_scalar(T.off[:, 8 * d + t:8 * d + 8:2], T.ramp2[:, :], T.base[:, col:col + 1], None,
+                              AluOpType.add).then_inc(sem.vo, 1)
+    for b, v in enumerate(mine):
+        o = JW * b
+        for r in sorted(ranks, key=lambda x: (via[x][v] != x, T.rank_of(x))):
+            s = T.rank_of(r)
+            vec.wait_ge(sem["a%d_%d" % (b, s)], 4)
+            vec.transpose(T.win[:, o + W * s:o + W * s + W], T.lin[:, o + W * s:o + W * s + W]).then_inc(sem["vw%d" % b], 1)
+        if b == 0:
+            vec.wait_ge(sem.vo, 2 * NR)
+        vec.wait_ge(sem["vw%d" % b], NR)
+        for i in range(4):
+            ch = chips[(q + i) % 4]
+            ds = [T.rank_of(r) for r in ranks if topo.chip(r) == ch]
+            for d in ds:
+                vec.tensor_copy(T.gat[:, o + W * d:o + W * d + W],
+                                T.win[:, o:o + JW].indirect(T.off[:, 8 * d:8 * d + 8])).then_inc(sem["gd%d_%d" % (b, d)], 1)
+            for d in ds:
+                vec.wait_ge(sem["gd%d_%d" % (b, d)], 1)
+                vec.transpose(T.outb[:, o + W * d:o + W * d + W],
+                              T.gat[:, o + W * d:o + W * d + W]).then_inc(sem["td%d_%d" % (b, d)], 1)
+            for d in ds:
+                g.wait_ge(sem["td%d_%d" % (b, d)], 1)
+            g.remote_dma_fused([_tr(topo, ranks[d], T.outb[:, o + W * d:o + W * d + W], T.land[v], lo[4 * j:4 * j + 4],
+                                    sem["r%d" % v]) for j, d in enumerate(ds)], local_sem=sem.sent)
+            sent += 8
     g.wait_ge(sem.sent, sent)
 
 

from concourse.bass import DstId, RemoteDMATransfer
from concourse.mybir import AluOpType

SIM_CORES = 128
NR, NB, S = 8, 16, 256
NV = 32
RD = NV // 4
W = 128
JW = NR * W
HW = NR // 2

SCRATCH = {
    "stage": ("dram", [NV, 128, W], "float32"),
    "land": ("dram", [NV, 128, W], "float32"),
    "rep": ("sbuf", [128, 2 * NR], "int32"),
    "hi": ("sbuf", [128, 2 * NR], "int32"),
    "hif": ("sbuf", [128, 2 * NR], "float32"),
    "repf": ("sbuf", [128, 2 * NR], "float32"),
    "base": ("sbuf", [128, 2 * NR], "float32"),
    "pidx": ("sbuf", [128, 4], "int32"),
    "pbit": ("sbuf", [128, 4], "int32"),
    "pbf": ("sbuf", [128, 4], "float32"),
    "ramp": ("sbuf", [128, 4], "float32"),
    "ramp2": ("sbuf", [128, 4], "float32"),
    "off": ("sbuf", [128, 8 * NR], "uint16"),
    "lin": ("sbuf", [128, 2 * JW], "float32"),
    "win": ("sbuf", [128, 2 * JW], "float32"),
    "gat": ("sbuf", [128, 2 * JW], "float32"),
    "outb": ("sbuf", [128, 2 * JW], "float32"),
}
SEMAPHORES = (["psem", "pa", "pb", "vi", "vp", "vs", "vo", "vw0", "vw1", "sent", "ys", "yc", "go", "go2"]
              + ["f%d" % k for k in range(RD)] + ["ld%d" % k for k in range(RD)]
              + ["a%d_%d" % (b, s) for b in range(2) for s in range(NR)] + ["r%d" % v for v in range(NV)]
              + ["gd%d_%d" % (b, d) for b in range(2) for d in range(NR)]
              + ["td%d_%d" % (b, d) for b in range(2) for d in range(NR)])


def _bits(mask):
    return [b for b in range(mask.bit_length()) if (mask >> b) & 1]


def _mask(engines):
    m = 0
    for e in engines:
        m |= 1 << e
    return m


def _plan(T, topo):
    ranks = list(T.cores)
    cores = list(range(SIM_CORES))
    allchips = sorted({topo.chip(c) for c in cores})
    chips = []
    for r in ranks:
        if topo.chip(r) not in chips:
            chips.append(topo.chip(r))
    sorter, slots = {}, {}
    for q, ch in enumerate(chips):
        rdie = topo.die([r for r in ranks if topo.chip(r) == ch][0])
        mate = [x for x in allchips if topo.mates(ch, x)][0]
        cand = [c for c in cores if topo.chip(c) == mate and c not in ranks
                and all(topo.may_write(c, r) for r in ranks)]
        slots[q] = [c for c in cand if topo.die(c) == rdie][:2] + [c for c in cand if topo.die(c) != rdie][:2]
        for i in range(RD):
            k = i % 4
            sorter[4 * i + q] = slots[q][2 * ((k + q) % 2) + k // 2]
    via, fwd = {}, {}
    for ch in chips:
        here = [r for r in ranks if topo.chip(r) == ch]
        rdie = topo.die(here[0])
        helpers = [c for c in cores if topo.chip(c) == ch and c not in ranks and topo.die(c) != rdie
                   and all(topo.may_write(c, sorter[v]) for v in sorter)]
        for e, r in enumerate(here):
            fwd[r] = helpers[e]
            via[r] = {}
            for i in range(RD):
                for q in range(4):
                    via[r][4 * i + q] = r if (i + q + e) % 2 == 0 else helpers[e]
    return ranks, chips, sorter, slots, via, fwd


def _tr(topo, dst, src_ap, dst_ap, engines, sem):
    rid, pid, _ = topo.addr(dst)
    return RemoteDMATransfer(dst_ids=[DstId(rid=rid, pnc=pid)], dma_engine_mask=_mask(engines), remote_sem=sem,
                             src=src_ap, dst=dst_ap)


def _lin(T, v, s):
    a = JW * (v // (NV // 2)) + W * s
    return T.lin[:, a:a + W]


def _rank(g, core, T, topo, ranks, chips, sorter, slots, via, fwd):
    sem = T.sem
    s = T.rank_of(core)
    q = chips.index(topo.chip(core))
    e = [r for r in ranks if topo.chip(r) == topo.chip(core)].index(core)
    lo = _bits(topo.mask(core, sorter[0]))
    hi = [b for b in _bits(topo.mask(core, fwd[core])) if b not in lo]
    sent = 0
    n = 0
    for grp in range(8):
        for t in range(2):
            for two in range(2):
                (g.sync, g.scalar)[n % 2].dma_start(
                    T.rep[16 * grp + two:16 * grp + 16:2, 2 * HW * e + HW * t:2 * HW * e + HW * t + HW],
                    T.parent[8 * t:8 * t + 8, HW * e:HW * e + HW]).then_inc(sem.psem, 16)
                n += 1

    def load(i):
        g.sync.dma_start(T.stage[4 * i:4 * i + 4], T.c[16 * i:16 * i + 16, :]).then_inc(sem["ld%d" % i], 16)

    for i in range(RD // 2):
        load(i)
    g.sync.wait_ge(sem.go, 1)
    for i in range(RD // 2, RD):
        load(i)
    g.sync.sem_inc(sem.go2, 1)
    g.wait_ge(sem.psem, 16 * n)
    half = T.rep[:, 2 * HW * e:2 * HW * e + 2 * HW]
    g.remote_dma_fused([_tr(topo, slots[q][e], half, half, lo, sem.pa),
                        _tr(topo, fwd[core], half, half, hi, sem.pa)], local_sem=sem.sent)
    sent += 16
    for i in range(RD):
        g.wait_ge(sem["ld%d" % i], 16)
        vs = [4 * i + (q + j) % 4 for j in range(4)]
        far = [v for v in vs if via[core][v] != core]
        near = [v for v in vs if via[core][v] == core]
        g.remote_dma_fused([_tr(topo, fwd[core], T.stage[v], T.stage[v], hi[4 * j:4 * j + 4], sem["f%d" % i])
                            for j, v in enumerate(far)]
                           + [_tr(topo, sorter[v], T.stage[v], _lin(T, v, s), lo[4 * j:4 * j + 4],
                                  sem["a%d_%d" % (v // (NV // 2), s)]) for j, v in enumerate(near)], local_sem=sem.sent)
        sent += 16
        if i == 1:
            g.sem_inc(sem.go, 1)
            g.wait_ge(sem.go2, 1)
    for queue, z, done in ((g.sync, 0, sem.ys), (g.scalar, 1, sem.yc)):
        for i in range(RD):
            a = 4 * i + 2 * z
            queue.wait_ge(sem["r%d" % a], 4)
            queue.wait_ge(sem["r%d" % (a + 1)], 4)
            queue.dma_start(T.y[4 * a:4 * a + 8, :], T.land[a:a + 2]).then_inc(done, 16)
        queue.wait_ge(done, 16 * RD)
    g.wait_ge(sem.sent, sent)


def _forwarder(g, core, T, topo, ranks, chips, sorter, slots, via, fwd):
    sem = T.sem
    r = [x for x in ranks if fwd[x] == core][0]
    s = T.rank_of(r)
    q = chips.index(topo.chip(core))
    e = [x for x in ranks if topo.chip(x) == topo.chip(core)].index(r)
    lo = _bits(topo.mask(core, sorter[0]))
    sent = 0
    half = T.rep[:, 2 * HW * e:2 * HW * e + 2 * HW]
    g.wait_ge(sem.pa, 8)
    g.remote_dma_fused([_tr(topo, slots[q][2 + e], half, half, lo, sem.pa)], local_sem=sem.sent)
    sent += 8
    for i in range(RD):
        far = [4 * i + (q + j) % 4 for j in range(4) if via[r][4 * i + (q + j) % 4] == core]
        g.wait_ge(sem["f%d" % i], 8)
        g.remote_dma_fused([_tr(topo, sorter[v], T.stage[v], _lin(T, v, s), lo[4 * j:4 * j + 4],
                                sem["a%d_%d" % (v // (NV // 2), s)]) for j, v in enumerate(far)], local_sem=sem.sent)
        sent += 8
    g.wait_ge(sem.sent, sent)


def _sorter(g, core, T, topo, ranks, chips, sorter, slots, via):
    sem = T.sem
    mine = sorted(x for x in sorter if sorter[x] == core)
    q = mine[0] % 4
    lo = _bits(topo.mask(core, ranks[0]))
    vec = g.vector
    g.iota(T.ramp[:, :], [[32, 4]], 0, 0, allow_small_or_imprecise_dtypes=True).then_inc(sem.vi, 1)
    g.iota(T.pidx[:, :], [[0, 4]], 0, 1).then_inc(sem.vi, 1)
    vec.wait_ge(sem.vi, 2)
    vec.tensor_scalar(T.pbit[:, :], T.pidx[:, :], 1, None, AluOpType.bitwise_and).then_inc(sem.vp, 1)
    vec.wait_ge(sem.vp, 1)
    vec.tensor_copy(T.pbf[:, :], T.pbit[:, :]).then_inc(sem.vp, 1)
    vec.wait_ge(sem.vp, 2)
    vec.tensor_tensor(T.ramp2[:, :], T.ramp[:, :], T.pbf[:, :], AluOpType.add).then_inc(sem.vp, 1)
    sl = slots[q].index(core)
    e = sl % 2
    half = T.rep[:, 2 * HW * e:2 * HW * e + 2 * HW]
    g.wait_ge(sem.pa, 8)
    g.remote_dma_fused([_tr(topo, slots[q][sl - e + 1 - e], half, half, lo, sem.pb)], local_sem=sem.sent)
    sent = 8
    vec.wait_ge(sem.pa, 8)
    vec.wait_ge(sem.pb, 8)
    vec.tensor_scalar(T.hi[:, :], T.rep[:, :], 4, None, AluOpType.arith_shift_right).then_inc(sem.vs, 1)
    vec.tensor_scalar(T.repf[:, :], T.rep[:, :], 2, None, AluOpType.mult).then_inc(sem.vs, 1)
    vec.wait_ge(sem.vs, 2)
    vec.tensor_scalar(T.hif[:, :], T.hi[:, :], W - 2 * NB, None, AluOpType.mult).then_inc(sem.vs, 1)
    vec.wait_ge(sem.vs, 3)
    vec.tensor_tensor(T.base[:, :], T.hif[:, :], T.repf[:, :], AluOpType.add).then_inc(sem.vs, 1)
    vec.wait_ge(sem.vs, 4)
    vec.wait_ge(sem.vp, 3)
    for d in range(NR):
        for t in range(2):
            col = 2 * HW * (d // HW) + HW * t + d % HW
            vec.tensor_scalar(T.off[:, 8 * d + t:8 * d + 8:2], T.ramp2[:, :], T.base[:, col:col + 1], None,
                              AluOpType.add).then_inc(sem.vo, 1)
    for b, v in enumerate(mine):
        o = JW * b
        for r in sorted(ranks, key=lambda x: (via[x][v] != x, T.rank_of(x))):
            s = T.rank_of(r)
            vec.wait_ge(sem["a%d_%d" % (b, s)], 4)
            vec.transpose(T.win[:, o + W * s:o + W * s + W], T.lin[:, o + W * s:o + W * s + W]).then_inc(sem["vw%d" % b], 1)
        if b == 0:
            vec.wait_ge(sem.vo, 2 * NR)
        vec.wait_ge(sem["vw%d" % b], NR)
        for i in range(4):
            ch = chips[(q + i) % 4]
            ds = [T.rank_of(r) for r in ranks if topo.chip(r) == ch]
            for d in ds:
                vec.tensor_copy(T.gat[:, o + W * d:o + W * d + W],
                                T.win[:, o:o + JW].indirect(T.off[:, 8 * d:8 * d + 8])).then_inc(sem["gd%d_%d" % (b, d)], 1)
            for d in ds:
                vec.wait_ge(sem["gd%d_%d" % (b, d)], 1)
                vec.transpose(T.outb[:, o + W * d:o + W * d + W],
                              T.gat[:, o + W * d:o + W * d + W]).then_inc(sem["td%d_%d" % (b, d)], 1)
            for d in ds:
                g.wait_ge(sem["td%d_%d" % (b, d)], 1)
            g.remote_dma_fused([_tr(topo, ranks[d], T.outb[:, o + W * d:o + W * d + W], T.land[v], lo[4 * j:4 * j + 4],
                                    sem["r%d" % v]) for j, d in enumerate(ds)], local_sem=sem.sent)
            sent += 8
    g.wait_ge(sem.sent, sent)


def rank_program(g, core, T, topo):
    ranks, chips, sorter, slots, via, fwd = _plan(T, topo)
    if core in ranks:
        _rank(g, core, T, topo, ranks, chips, sorter, slots, via, fwd)
    elif core in fwd.values():
        _forwarder(g, core, T, topo, ranks, chips, sorter, slots, via, fwd)
    elif core in sorter.values():
        _sorter(g, core, T, topo, ranks, chips, sorter, slots, via)
